import numpy as np
import ml_dtypes


def mxq(x, axis, fmt="e4m3"):
    dtype, down = {"e4m3": (ml_dtypes.float8_e4m3fn, 7), "e5m2": (ml_dtypes.float8_e5m2, 14)}[fmt]
    v = np.moveaxis(np.asarray(x, np.float32).astype(ml_dtypes.bfloat16).astype(np.float64), axis, -1)
    blocks = v.reshape(v.shape[:-1] + (-1, 32))
    amax = np.abs(blocks).max(-1, keepdims=True)
    byte = np.maximum(np.where(amax > 0, np.frexp(amax)[1] - 1 + 127, 0) - down, 1)
    scale = np.exp2(byte - 127.0)
    codes = (blocks / scale).astype(np.float32).astype(dtype).astype(np.float64)
    return np.moveaxis((codes * scale).reshape(v.shape), -1, axis)


WIDE = False


def mx_kscale(k):
    if not WIDE:
        return np.ones(k)
    levels = np.array([10, -10, 5, -5, 0])
    if k % 512:
        return np.exp2(np.random.permutation(np.resize(levels, k // 32))).repeat(32)
    a = np.empty((k // 512, 16))
    for p in range(k // 512):
        a[p, :8] = np.random.permutation(np.resize(levels, 8))
        for g in range(8):
            far = levels[np.abs(levels - a[p, g]) >= 10]
            a[p, g + 8] = far[np.random.randint(len(far))]
    return np.exp2(a.ravel()).repeat(32)


def f64(x):
    return np.asarray(x).astype(np.float64)


def striped(idx):
    return np.tile(idx.reshape(-1, 16).T, (8, 1)).astype(np.uint16)


def unstriped(offs):
    return offs[:16].T.reshape(-1).astype(np.int64)


E2M1 = np.array([0.0, 0.5, 1.0, 1.5, 2.0, 3.0, 4.0, 6.0, -0.0, -0.5, -1.0, -1.5, -2.0, -3.0, -4.0, -6.0])


def pack_weight(w, fmt):
    k, n = w.shape
    w = f64(np.asarray(w, np.float32).astype(ml_dtypes.bfloat16)).reshape(k // 32, 32, n)
    amax = np.abs(w).max(1)
    if fmt == "e4m3":
        byte = np.frexp(amax)[1] - 1 + 127 - 7
    else:
        mant, ex = np.frexp(amax / 6.0)
        byte = np.where(mant > 0.5, ex, ex - 1) + 127
    byte = np.clip(np.where(amax > 0, byte, 1), 1, 254)
    scaled = (w * np.exp2(127.0 - byte)[:, None, :]).reshape(k, n).astype(np.float32)
    by_word = np.ascontiguousarray(scaled.reshape(k // 512, 128, 4, n).transpose(0, 1, 3, 2))
    if fmt == "e4m3":
        words = by_word.astype(ml_dtypes.float8_e4m3fn).view(np.uint8)
    else:
        c = by_word.astype(ml_dtypes.float4_e2m1fn).view(np.uint8) & 0xF
        words = (c[..., 0::2] | (c[..., 1::2] << 4)).reshape(k // 512, 128, 2 * n)
    return np.ascontiguousarray(words), np.ascontiguousarray(byte.astype(np.uint8).reshape(k // 512, 16, n))


def unpack_weight(words, scales, fmt):
    g, _, n = scales.shape
    words = np.ascontiguousarray(words).reshape(g, 128, n, -1)
    if fmt == "e4m3":
        vals = words.view(ml_dtypes.float8_e4m3fn).astype(np.float64)
    else:
        nib = np.empty((g, 128, n, 4), np.uint8)
        nib[..., 0::2] = words & 0xF
        nib[..., 1::2] = words >> 4
        vals = E2M1[nib]
    vals = vals * np.repeat(np.exp2(scales.astype(np.float64) - 127.0), 8, axis=1)[..., None]
    return vals.transpose(0, 1, 3, 2).reshape(g * 512, n)


def gelu(v):
    return 0.5 * v * (1.0 + np.tanh(np.sqrt(2.0 / np.pi) * (v + 0.044715 * v**3)))


K, T, S, S2 = 1024, 2048, 512, 1024

def setup_inputs():
    n = np.random.standard_normal
    s = mx_kscale(K)[:, None]
    d = {}
    d["tab_words"], d["tab_scales"] = pack_weight(n((K, T)) * s, "e4m3")
    d["w1"] = (n((K, K)) / K / s / s.T).astype(np.float32)
    d["w2_words"], d["w2_scales"] = pack_weight(1.2 * n((K, K)) / K / s / s.T, "e2m1")
    d["bias"] = (0.7 * n(K) / K ** 0.5 / s[:, 0]).astype(np.float32)
    d["lean"] = np.random.uniform(0.5, 2.0, S2).astype(np.float32)
    d["offs"] = striped(np.random.permutation(T)[:S])
    d["offs2"] = striped(np.random.permutation(T)[:S2])
    return d

def reference(tab_words, tab_scales, w1, w2_words, w2_scales, bias, lean, offs, offs2):
    TW = unpack_weight(tab_words, tab_scales, "e4m3")
    v = TW[:, unstriped(offs)]
    v2 = TW[:, unstriped(offs2)]
    w2 = unpack_weight(w2_words, w2_scales, "e2m1")
    h1 = np.abs(mxq(f64(w1), 0, "e4m3").T @ v)
    h2 = np.maximum((w2.T @ v) + f64(bias)[:, None], 0.0)
    e1 = v2.T @ mxq(h1, 0, "e4m3")
    e2 = v2.T @ mxq(h2, 0, "e4m3")
    return e1 * e2 + f64(lean)[:, None] * e1 + e2

@@ -1,0 +1,258 @@
+from contextlib import ExitStack
+
+import concourse.mybir as mybir
+
+K, T, S, S2 = 1024, 2048, 512, 1024
+FLOPS = 2 * K * K * S * 2 + 2 * K * S2 * S * 2
+
+F32 = mybir.dt.float32
+BF16 = mybir.dt.bfloat16
+I32 = mybir.dt.int32
+U32 = mybir.dt.uint32
+U16 = mybir.dt.uint16
+U8 = mybir.dt.uint8
+FP8X4 = mybir.dt.float8_e4m3fn_x4
+FP4X4 = mybir.dt.float4_e2m1fn_x4
+ACT = mybir.ActivationFunctionType
+ALU = mybir.AluOpType
+
+P = 128
+PACK = 4
+KP = P * PACK
+PASSES = K // KP
+JC = 128
+HALF = 512
+G_TILES = 5
+
+
+def tile_list_cask_harmony_scores_kernel(
+    tc, tab_words, tab_scales, w1, w2_words, w2_scales, bias, lean, offs, offs2, out
+):
+    nc = tc.nc
+    with ExitStack() as ctx:
+        lists = ctx.enter_context(tc.tile_pool(name="lists", bufs=1))
+        keep = ctx.enter_context(tc.tile_pool(name="keep", bufs=1))
+        psum = ctx.enter_context(tc.psum_pool(name="psum", bufs=1))
+
+        def held(shape, dtype, name, tag=None):
+            return keep.tile(shape, dtype, name=name, tag=tag or name, align_bytes=64)
+
+        banks_taken = []
+
+        def next_bank(shape):
+            tag = f"bank{len(banks_taken) % 8}"
+            banks_taken.append(tag)
+            return psum.tile(shape, F32, name=tag, tag=tag)
+
+        cand_list = lists.tile([P, S // 16], U16, name="cand_list")
+        base_list = lists.tile([P, S2 // 16], U16, name="base_list")
+
+        tab_sc = held([P, T], U8, "tab_sc")
+        w2_sc_raw = held([P, PASSES, K], U8, "w2_sc_raw")
+        cand_sc1 = held([P, S], U8, "cand_sc1")
+        nc.gpsimd.memset(tab_sc[:].bitcast(I32), 0)
+        nc.vector.memset(w2_sc_raw[:].bitcast(I32), 0)
+        nc.vector.memset(cand_sc1[:].bitcast(I32), 0)
+
+        w2_raw = held([P, PASSES, K], U16, "w2_raw")
+        nc.sync.dma_start(cand_list[:], offs)
+        for q in range(4):
+            nc.sync.dma_start(
+                out=tab_sc[32 * q : 32 * q + 8, :].bitcast(I32),
+                in_=tab_scales[:, 4 * q : 4 * q + 4, :].bitcast(I32),
+            )
+
+        cand_sc = held([P, S], U8, "cand_sc")
+        nc.vector.tensor_copy(out=cand_sc[:], in_=tab_sc[:].indirect(cand_list[:]))
+        nc.sync.dma_start(out=cand_sc1[0:112, :].bitcast(I32), in_=cand_sc[4:116, :].bitcast(I32))
+        nc.sync.dma_start(base_list[:], offs2)
+        nc.sync.dma_start(out=w2_raw[:].bitcast(I32), in_=w2_words.rearrange("a p c -> p a c").bitcast(I32))
+        tab_w = [held([P, T], I32, f"tab_w{a}") for a in range(PASSES)]
+        w1_raw = {}
+
+        def load_w1(a, b):
+            w1_raw[a, b] = held([P, PACK, KP], F32, f"w1_raw{a}{b}")
+            nc.sync.dma_start(
+                out=w1_raw[a, b][:],
+                in_=w1[KP * a : KP * (a + 1), KP * b : KP * (b + 1)].rearrange("(p j) c -> p j c", j=PACK),
+            )
+
+        def load_tab(a):
+            nc.sync.dma_start(out=tab_w[a][:], in_=tab_words[a].rearrange("p t i -> p (t i)").bitcast(I32))
+
+        bias_t = held([P, PASSES, PACK], F32, "bias_t")
+        lean_t = held([P, S2 // P], F32, "lean_t")
+        load_tab(0)
+        for q in range(4):
+            nc.sync.dma_start(
+                out=w2_sc_raw[32 * q : 32 * q + 4, :, :].bitcast(I32),
+                in_=w2_scales[:, 4 * q : 4 * q + 4, :].rearrange("a r c -> r a c").bitcast(I32),
+            )
+        load_tab(1)
+        load_w1(0, 0)
+        load_w1(1, 0)
+        nc.sync.dma_start(out=bias_t[:], in_=bias.rearrange("(b p t) -> p b t", p=P, t=PACK))
+        load_w1(0, 1)
+        load_w1(1, 1)
+        with nc.allow_non_contiguous_dma(reason="one value of lean to a partition"):
+            nc.sync.dma_start(out=lean_t[:], in_=lean.rearrange("(m p) -> p m", p=P))
+
+        w2_w = held([P, PASSES, K], U16, "w2_w")
+        w2_sc = held([P, PASSES, K], U8, "w2_sc")
+        cand_w = [held([P, S], U32, f"cand_w{a}") for a in range(PASSES)]
+        base_w = {}
+        base_sc = [held([P, HALF], U8, f"base_sc{h}") for h in range(S2 // HALF)]
+
+        def gather_cand(a):
+            nc.vector.tensor_copy(out=cand_w[a][:], in_=tab_w[a][:].bitcast(U32).indirect(cand_list[:]))
+
+        def base_offsets(h):
+            return base_list[:, h * HALF // 16 : (h + 1) * HALF // 16]
+
+        def gather_base(a, h, tag=None):
+            base_w[a, h] = held([P, HALF], U32, f"base_w{a}{h}", tag)
+            nc.vector.tensor_copy(out=base_w[a, h][:], in_=tab_w[a][:].bitcast(U32).indirect(base_offsets(h)))
+
+        def gather_base_scales(h):
+            nc.vector.tensor_copy(out=base_sc[h][:], in_=tab_sc[:].indirect(base_offsets(h)))
+
+        w1_bf, w1_w, w1_sc = {}, {}, {}
+
+        def round_w1(a, b, on_vector):
+            w1_bf[a, b] = held([P, PACK, P, PACK], BF16, f"w1_bf{a}{b}")
+            dst = w1_bf[a, b][:].rearrange("p t m j -> p m j t")
+            src = w1_raw[a, b][:].rearrange("p j (m t) -> p m j t", t=PACK)
+            if on_vector:
+                nc.vector.tensor_copy(out=dst, in_=src)
+            else:
+                nc.scalar.activation(out=dst, in_=src, func=ACT.Copy)
+
+        def quantize(src, name):
+            words = held([P, KP], U32, name + "_w")
+            scales = held([P, KP], U8, name + "_sc")
+            nc.vector.quantize_mx(out=words[:].bitcast(FP8X4), scales=scales[:], in_=src)
+            return words, scales
+
+        def quantize_w1(a, b):
+            w1_w[a, b], w1_sc[a, b] = quantize(w1_bf[a, b][:].rearrange("p t m j -> p (t m j)"), f"w1q{a}{b}")
+
+        h_w, h_sc = {}, {}
+
+        def make_h2(b):
+            planes = held([P, PACK, S], BF16, f"h2_planes{b}")
+            for t in range(PACK):
+                bank = next_bank([P, S])
+                cols = slice(KP * b + P * t, KP * b + P * (t + 1))
+                for a in range(PASSES):
+                    nc.tensor.matmul_mx(
+                        out=bank[:],
+                        lhsT=w2_w[:, a, cols].bitcast(FP4X4),
+                        lhsT_scale=w2_sc[:, a, cols],
+                        rhs=cand_w[a][:].bitcast(FP8X4),
+                        rhs_scale=(cand_sc if a == 0 else cand_sc1)[:],
+                        start=(a == 0),
+                        stop=(a == PASSES - 1),
+                    )
+                nc.scalar.activation(out=planes[:, t, :], in_=bank[:], func=ACT.Relu, bias=bias_t[:, b, t : t + 1])
+            woven = held([P, S, PACK], BF16, f"h2_bf{b}")
+            nc.vector.tensor_copy(
+                out=woven[:].rearrange("p (c i) t -> p c t i", i=4),
+                in_=planes[:].rearrange("p t (c i) -> p c t i", i=4),
+            )
+            h_w[2, b], h_sc[2, b] = quantize(woven[:].rearrange("p j t -> p (j t)"), f"h2q{b}")
+
+        def make_h1(b):
+            woven = held([P, S, PACK], BF16, f"h1_bf{b}")
+            for c in range(S // JC):
+                bank = next_bank([P, PACK, JC])
+                jcols = slice(JC * c, JC * (c + 1))
+                for t in range(PACK):
+                    cols = slice(P * t, P * (t + 1))
+                    for a in range(PASSES):
+                        nc.tensor.matmul_mx(
+                            out=bank[:, t, :],
+                            lhsT=w1_w[a, b][:, cols].bitcast(FP8X4),
+                            lhsT_scale=w1_sc[a, b][:, cols],
+                            rhs=cand_w[a][:, jcols].bitcast(FP8X4),
+                            rhs_scale=cand_sc[4 * a : P, jcols],
+                            start=(a == 0),
+                            stop=(a == PASSES - 1),
+                        )
+                nc.scalar.activation(out=woven[:, jcols, :], in_=bank[:].rearrange("p t n -> p n t"), func=ACT.Abs)
+            h_w[1, b], h_sc[1, b] = quantize(woven[:].rearrange("p j t -> p (j t)"), f"h1q{b}")
+
+        def match(which, mt):
+            bank = next_bank([P, S])
+            h, cols = divmod(P * mt, HALF)
+            cols = slice(cols, cols + P)
+            for a in range(PASSES):
+                nc.tensor.matmul_mx(
+                    out=bank[:],
+                    lhsT=base_w[a, h][:, cols].bitcast(FP8X4),
+                    lhsT_scale=base_sc[h][4 * a : P, cols],
+                    rhs=h_w[which, a][:].bitcast(FP8X4),
+                    rhs_scale=h_sc[which, a][:],
+                    start=(a == 0),
+                    stop=(a == PASSES - 1),
+                )
+            return bank
+
+        round_w1(0, 0, False)
+        round_w1(1, 0, False)
+        gather_base_scales(0)
+        nc.vector.tensor_copy(
+            out=w2_w[:].rearrange("p a (b t m) -> p (a b) t m", t=PACK, m=P),
+            in_=w2_raw[:].rearrange("p a (b m t) -> p (a b) t m", t=PACK, m=P),
+        )
+        gather_base_scales(1)
+        nc.vector.tensor_copy(
+            out=w2_sc[:].rearrange("p a (b t m) -> p (a b) t m", t=PACK, m=P),
+            in_=w2_sc_raw[:].rearrange("p a (b m t) -> p (a b) t m", t=PACK, m=P),
+        )
+
+        quantize_w1(0, 0)
+        quantize_w1(1, 0)
+        gather_cand(0)
+        gather_cand(1)
+        round_w1(0, 1, True)
+        quantize_w1(0, 1)
+        round_w1(1, 1, True)
+        quantize_w1(1, 1)
+        make_h2(0)
+        make_h2(1)
+        make_h1(0)
+        make_h1(1)
+        gather_base(0, 0)
+        gather_base(1, 0)
+        gather_base(0, 1)
+        gather_base(1, 1, "h2_bf1")
+
+        e2_sb = {}
+
+        def match_e2(mt):
+            e2_sb[mt] = held([P, S], F32, f"e2_sb{mt}")
+            nc.scalar.activation(out=e2_sb[mt][:], in_=match(2, mt)[:], func=ACT.Copy)
+
+        for mt in range(4):
+            match_e2(mt)
+        for mt in range(S2 // P):
+            if mt not in e2_sb:
+                match_e2(mt)
+            e1_bank = match(1, mt)
+            prod = held([P, S], F32, f"prod{mt}")
+            result = held([P, S], F32, f"result{mt}")
+            if mt < G_TILES:
+                nc.vector.scalar_tensor_tensor(
+                    out=prod[:], in0=e2_sb[mt][:], scalar=lean_t[:, mt : mt + 1], in1=e1_bank[:],
+                    op0=ALU.add, op1=ALU.mult,
+                )
+                nc.gpsimd.tensor_tensor(out=result[:], in0=prod[:], in1=e2_sb[mt][:], op=ALU.add)
+            else:
+                nc.vector.scalar_tensor_tensor(
+                    out=prod[:], in0=e1_bank[:], scalar=1.0, in1=e2_sb[mt][:], op0=ALU.add, op1=ALU.mult,
+                )
+                nc.vector.scalar_tensor_tensor(
+                    out=result[:], in0=e1_bank[:], scalar=lean_t[:, mt : mt + 1], in1=prod[:],
+                    op0=ALU.mult, op1=ALU.add,
+                )
+            nc.sync.dma_start(out=out[P * mt : P * (mt + 1), :], in_=result[:])

@@ -22,7 +22,7 @@ KP = P * PACK
 PASSES = K // KP
 JC = 128
 HALF = 512
-G_TILES = 5
+G_TILES = 0
 
 
 def tile_list_cask_harmony_scores_kernel(

from contextlib import ExitStack

import concourse.mybir as mybir

K, T, S, S2 = 1024, 2048, 512, 1024
FLOPS = 2 * K * K * S * 2 + 2 * K * S2 * S * 2

F32 = mybir.dt.float32
BF16 = mybir.dt.bfloat16
I32 = mybir.dt.int32
U32 = mybir.dt.uint32
U16 = mybir.dt.uint16
U8 = mybir.dt.uint8
FP8X4 = mybir.dt.float8_e4m3fn_x4
FP4X4 = mybir.dt.float4_e2m1fn_x4
ACT = mybir.ActivationFunctionType
ALU = mybir.AluOpType

P = 128
PACK = 4
KP = P * PACK
PASSES = K // KP
JC = 128
HALF = 512
G_TILES = 0


def tile_list_cask_harmony_scores_kernel(
    tc, tab_words, tab_scales, w1, w2_words, w2_scales, bias, lean, offs, offs2, out
):
    nc = tc.nc
    with ExitStack() as ctx:
        lists = ctx.enter_context(tc.tile_pool(name="lists", bufs=1))
        keep = ctx.enter_context(tc.tile_pool(name="keep", bufs=1))
        psum = ctx.enter_context(tc.psum_pool(name="psum", bufs=1))

        def held(shape, dtype, name, tag=None):
            return keep.tile(shape, dtype, name=name, tag=tag or name, align_bytes=64)

        banks_taken = []

        def next_bank(shape):
            tag = f"bank{len(banks_taken) % 8}"
            banks_taken.append(tag)
            return psum.tile(shape, F32, name=tag, tag=tag)

        cand_list = lists.tile([P, S // 16], U16, name="cand_list")
        base_list = lists.tile([P, S2 // 16], U16, name="base_list")

        tab_sc = held([P, T], U8, "tab_sc")
        w2_sc_raw = held([P, PASSES, K], U8, "w2_sc_raw")
        cand_sc1 = held([P, S], U8, "cand_sc1")
        nc.gpsimd.memset(tab_sc[:].bitcast(I32), 0)
        nc.vector.memset(w2_sc_raw[:].bitcast(I32), 0)
        nc.vector.memset(cand_sc1[:].bitcast(I32), 0)

        w2_raw = held([P, PASSES, K], U16, "w2_raw")
        nc.sync.dma_start(cand_list[:], offs)
        for q in range(4):
            nc.sync.dma_start(
                out=tab_sc[32 * q : 32 * q + 8, :].bitcast(I32),
                in_=tab_scales[:, 4 * q : 4 * q + 4, :].bitcast(I32),
            )

        cand_sc = held([P, S], U8, "cand_sc")
        nc.vector.tensor_copy(out=cand_sc[:], in_=tab_sc[:].indirect(cand_list[:]))
        nc.sync.dma_start(out=cand_sc1[0:112, :].bitcast(I32), in_=cand_sc[4:116, :].bitcast(I32))
        nc.sync.dma_start(base_list[:], offs2)
        nc.sync.dma_start(out=w2_raw[:].bitcast(I32), in_=w2_words.rearrange("a p c -> p a c").bitcast(I32))
        tab_w = [held([P, T], I32, f"tab_w{a}") for a in range(PASSES)]
        w1_raw = {}

        def load_w1(a, b):
            w1_raw[a, b] = held([P, PACK, KP], F32, f"w1_raw{a}{b}")
            nc.sync.dma_start(
                out=w1_raw[a, b][:],
                in_=w1[KP * a : KP * (a + 1), KP * b : KP * (b + 1)].rearrange("(p j) c -> p j c", j=PACK),
            )

        def load_tab(a):
            nc.sync.dma_start(out=tab_w[a][:], in_=tab_words[a].rearrange("p t i -> p (t i)").bitcast(I32))

        bias_t = held([P, PASSES, PACK], F32, "bias_t")
        lean_t = held([P, S2 // P], F32, "lean_t")
        load_tab(0)
        for q in range(4):
            nc.sync.dma_start(
                out=w2_sc_raw[32 * q : 32 * q + 4, :, :].bitcast(I32),
                in_=w2_scales[:, 4 * q : 4 * q + 4, :].rearrange("a r c -> r a c").bitcast(I32),
            )
        load_tab(1)
        load_w1(0, 0)
        load_w1(1, 0)
        nc.sync.dma_start(out=bias_t[:], in_=bias.rearrange("(b p t) -> p b t", p=P, t=PACK))
        load_w1(0, 1)
        load_w1(1, 1)
        with nc.allow_non_contiguous_dma(reason="one value of lean to a partition"):
            nc.sync.dma_start(out=lean_t[:], in_=lean.rearrange("(m p) -> p m", p=P))

        w2_w = held([P, PASSES, K], U16, "w2_w")
        w2_sc = held([P, PASSES, K], U8, "w2_sc")
        cand_w = [held([P, S], U32, f"cand_w{a}") for a in range(PASSES)]
        base_w = {}
        base_sc = [held([P, HALF], U8, f"base_sc{h}") for h in range(S2 // HALF)]

        def gather_cand(a):
            nc.vector.tensor_copy(out=cand_w[a][:], in_=tab_w[a][:].bitcast(U32).indirect(cand_list[:]))

        def base_offsets(h):
            return base_list[:, h * HALF // 16 : (h + 1) * HALF // 16]

        def gather_base(a, h, tag=None):
            base_w[a, h] = held([P, HALF], U32, f"base_w{a}{h}", tag)
            nc.vector.tensor_copy(out=base_w[a, h][:], in_=tab_w[a][:].bitcast(U32).indirect(base_offsets(h)))

        def gather_base_scales(h):
            nc.vector.tensor_copy(out=base_sc[h][:], in_=tab_sc[:].indirect(base_offsets(h)))

        w1_bf, w1_w, w1_sc = {}, {}, {}

        def round_w1(a, b, on_vector):
            w1_bf[a, b] = held([P, PACK, P, PACK], BF16, f"w1_bf{a}{b}")
            dst = w1_bf[a, b][:].rearrange("p t m j -> p m j t")
            src = w1_raw[a, b][:].rearrange("p j (m t) -> p m j t", t=PACK)
            if on_vector:
                nc.vector.tensor_copy(out=dst, in_=src)
            else:
                nc.scalar.activation(out=dst, in_=src, func=ACT.Copy)

        def quantize(src, name):
            words = held([P, KP], U32, name + "_w")
            scales = held([P, KP], U8, name + "_sc")
            nc.vector.quantize_mx(out=words[:].bitcast(FP8X4), scales=scales[:], in_=src)
            return words, scales

        def quantize_w1(a, b):
            w1_w[a, b], w1_sc[a, b] = quantize(w1_bf[a, b][:].rearrange("p t m j -> p (t m j)"), f"w1q{a}{b}")

        h_w, h_sc = {}, {}

        def make_h2(b):
            planes = held([P, PACK, S], BF16, f"h2_planes{b}")
            for t in range(PACK):
                bank = next_bank([P, S])
                cols = slice(KP * b + P * t, KP * b + P * (t + 1))
                for a in range(PASSES):
                    nc.tensor.matmul_mx(
                        out=bank[:],
                        lhsT=w2_w[:, a, cols].bitcast(FP4X4),
                        lhsT_scale=w2_sc[:, a, cols],
                        rhs=cand_w[a][:].bitcast(FP8X4),
                        rhs_scale=(cand_sc if a == 0 else cand_sc1)[:],
                        start=(a == 0),
                        stop=(a == PASSES - 1),
                    )
                nc.scalar.activation(out=planes[:, t, :], in_=bank[:], func=ACT.Relu, bias=bias_t[:, b, t : t + 1])
            woven = held([P, S, PACK], BF16, f"h2_bf{b}")
            nc.vector.tensor_copy(
                out=woven[:].rearrange("p (c i) t -> p c t i", i=4),
                in_=planes[:].rearrange("p t (c i) -> p c t i", i=4),
            )
            h_w[2, b], h_sc[2, b] = quantize(woven[:].rearrange("p j t -> p (j t)"), f"h2q{b}")

        def make_h1(b):
            woven = held([P, S, PACK], BF16, f"h1_bf{b}")
            for c in range(S // JC):
                bank = next_bank([P, PACK, JC])
                jcols = slice(JC * c, JC * (c + 1))
                for t in range(PACK):
                    cols = slice(P * t, P * (t + 1))
                    for a in range(PASSES):
                        nc.tensor.matmul_mx(
                            out=bank[:, t, :],
                            lhsT=w1_w[a, b][:, cols].bitcast(FP8X4),
                            lhsT_scale=w1_sc[a, b][:, cols],
                            rhs=cand_w[a][:, jcols].bitcast(FP8X4),
                            rhs_scale=cand_sc[4 * a : P, jcols],
                            start=(a == 0),
                            stop=(a == PASSES - 1),
                        )
                nc.scalar.activation(out=woven[:, jcols, :], in_=bank[:].rearrange("p t n -> p n t"), func=ACT.Abs)
            h_w[1, b], h_sc[1, b] = quantize(woven[:].rearrange("p j t -> p (j t)"), f"h1q{b}")

        def match(which, mt):
            bank = next_bank([P, S])
            h, cols = divmod(P * mt, HALF)
            cols = slice(cols, cols + P)
            for a in range(PASSES):
                nc.tensor.matmul_mx(
                    out=bank[:],
                    lhsT=base_w[a, h][:, cols].bitcast(FP8X4),
                    lhsT_scale=base_sc[h][4 * a : P, cols],
                    rhs=h_w[which, a][:].bitcast(FP8X4),
                    rhs_scale=h_sc[which, a][:],
                    start=(a == 0),
                    stop=(a == PASSES - 1),
                )
            return bank

        round_w1(0, 0, False)
        round_w1(1, 0, False)
        gather_base_scales(0)
        nc.vector.tensor_copy(
            out=w2_w[:].rearrange("p a (b t m) -> p (a b) t m", t=PACK, m=P),
            in_=w2_raw[:].rearrange("p a (b m t) -> p (a b) t m", t=PACK, m=P),
        )
        gather_base_scales(1)
        nc.vector.tensor_copy(
            out=w2_sc[:].rearrange("p a (b t m) -> p (a b) t m", t=PACK, m=P),
            in_=w2_sc_raw[:].rearrange("p a (b m t) -> p (a b) t m", t=PACK, m=P),
        )

        quantize_w1(0, 0)
        quantize_w1(1, 0)
        gather_cand(0)
        gather_cand(1)
        round_w1(0, 1, True)
        quantize_w1(0, 1)
        round_w1(1, 1, True)
        quantize_w1(1, 1)
        make_h2(0)
        make_h2(1)
        make_h1(0)
        make_h1(1)
        gather_base(0, 0)
        gather_base(1, 0)
        gather_base(0, 1)
        gather_base(1, 1, "h2_bf1")

        e2_sb = {}

        def match_e2(mt):
            e2_sb[mt] = held([P, S], F32, f"e2_sb{mt}")
            nc.scalar.activation(out=e2_sb[mt][:], in_=match(2, mt)[:], func=ACT.Copy)

        for mt in range(4):
            match_e2(mt)
        for mt in range(S2 // P):
            if mt not in e2_sb:
                match_e2(mt)
            e1_bank = match(1, mt)
            prod = held([P, S], F32, f"prod{mt}")
            result = held([P, S], F32, f"result{mt}")
            if mt < G_TILES:
                nc.vector.scalar_tensor_tensor(
                    out=prod[:], in0=e2_sb[mt][:], scalar=lean_t[:, mt : mt + 1], in1=e1_bank[:],
                    op0=ALU.add, op1=ALU.mult,
                )
                nc.gpsimd.tensor_tensor(out=result[:], in0=prod[:], in1=e2_sb[mt][:], op=ALU.add)
            else:
                nc.vector.scalar_tensor_tensor(
                    out=prod[:], in0=e1_bank[:], scalar=1.0, in1=e2_sb[mt][:], op0=ALU.add, op1=ALU.mult,
                )
                nc.vector.scalar_tensor_tensor(
                    out=result[:], in0=e1_bank[:], scalar=lean_t[:, mt : mt + 1], in1=prod[:],
                    op0=ALU.mult, op1=ALU.add,
                )
            nc.sync.dma_start(out=out[P * mt : P * (mt + 1), :], in_=result[:])
